import numpy as np
import ml_dtypes


def mxq(x, axis, fmt="e4m3"):
    dtype, down = {"e4m3": (ml_dtypes.float8_e4m3fn, 7), "e5m2": (ml_dtypes.float8_e5m2, 14)}[fmt]
    v = np.moveaxis(np.asarray(x, np.float32).astype(ml_dtypes.bfloat16).astype(np.float64), axis, -1)
    blocks = v.reshape(v.shape[:-1] + (-1, 32))
    amax = np.abs(blocks).max(-1, keepdims=True)
    byte = np.maximum(np.where(amax > 0, np.frexp(amax)[1] - 1 + 127, 0) - down, 1)
    scale = np.exp2(byte - 127.0)
    codes = (blocks / scale).astype(np.float32).astype(dtype).astype(np.float64)
    return np.moveaxis((codes * scale).reshape(v.shape), -1, axis)


WIDE = False


def mx_kscale(k):
    if not WIDE:
        return np.ones(k)
    levels = np.array([10, -10, 5, -5, 0])
    if k % 512:
        return np.exp2(np.random.permutation(np.resize(levels, k // 32))).repeat(32)
    a = np.empty((k // 512, 16))
    for p in range(k // 512):
        a[p, :8] = np.random.permutation(np.resize(levels, 8))
        for g in range(8):
            far = levels[np.abs(levels - a[p, g]) >= 10]
            a[p, g + 8] = far[np.random.randint(len(far))]
    return np.exp2(a.ravel()).repeat(32)


def f64(x):
    return np.asarray(x).astype(np.float64)


def striped(idx):
    return np.tile(idx.reshape(-1, 16).T, (8, 1)).astype(np.uint16)


def unstriped(offs):
    return offs[:16].T.reshape(-1).astype(np.int64)


def pack_weight(w):
    k, n = w.shape
    w = f64(np.asarray(w, np.float32).astype(ml_dtypes.bfloat16)).reshape(k // 32, 32, n)
    amax = np.abs(w).max(1)
    byte = np.clip(np.where(amax > 0, np.frexp(amax)[1] - 1 + 127 - 7, 1), 1, 254)
    scaled = (w * np.exp2(127.0 - byte)[:, None, :]).reshape(k, n).astype(np.float32)
    words = np.ascontiguousarray(scaled.reshape(k // 512, 128, 4, n).transpose(0, 1, 3, 2)).astype(ml_dtypes.float8_e4m3fn).view(np.uint8)
    return words, np.ascontiguousarray(byte.astype(np.uint8).reshape(k // 512, 16, n))


def unpack_weight(words, scales):
    g, p, n, _ = words.shape
    vals = np.ascontiguousarray(words).view(ml_dtypes.float8_e4m3fn).astype(np.float64) * np.repeat(np.exp2(scales.astype(np.float64) - 127.0), 8, axis=1)[..., None]
    return vals.transpose(0, 1, 3, 2).reshape(g * 512, n)

def planes(y):
    n, m = y.shape
    v = y.astype(np.float32).astype(ml_dtypes.bfloat16).astype(np.float64).reshape(n // 32, 32, m)
    top = np.abs(v).max(1)
    byte = np.clip(np.where(top > 0, np.frexp(top)[1] - 1 + 127 - 7, 1), 1, 254)
    codes = (v * np.exp2(127.0 - byte)[:, None, :]).reshape(n, m).astype(np.float32).astype(ml_dtypes.float8_e4m3fn).view(np.uint8)
    words = codes.reshape(n // 512, 128, 4, m).transpose(0, 1, 3, 2)
    return np.ascontiguousarray(words), np.ascontiguousarray(byte.astype(np.uint8).reshape(n // 512, 16, m))


K, T, S, D, V, N = 512, 1024, 512, 4, 256, 512
P = 2 ** 7


def setup_inputs():
    n = np.random.standard_normal
    s = mx_kscale(K)[:, None]
    packed_xT = pack_weight(n((K, T)) * s)
    return {
        "x_words": packed_xT[0],
        "x_scales": packed_xT[1],
        "w1": (n((K, N)) / np.sqrt(K) / s).astype(np.float32),
        "gate": (np.tile(np.random.uniform(0.2, 1.0, (D, 1, V)) / np.sqrt(D), (1, P, 1))).astype(np.float32),
        "offs": striped(np.random.permutation(T)[:S]),
        "cen": striped(np.random.permutation(S)[:V]),
        "pos1": striped(np.random.permutation(S)[:V]),
        "pos2": striped(np.random.permutation(S)[:V]),
        "pos3": striped(np.random.permutation(S)[:V]),
        "pos4": striped(np.random.permutation(S)[:V]),
    }


def reference(x_words, x_scales, w1, gate, offs, cen, pos1, pos2, pos3, pos4):
    xq = unpack_weight(x_words, x_scales)[:, unstriped(offs)]
    y = mxq(f64(w1), 0, "e4m3").T @ xq
    yc = y[:, unstriped(cen)]
    out_0 = yc + (y[:, unstriped(pos1)] - yc) * f64(gate)[0, :1] + (y[:, unstriped(pos2)] - yc) * f64(gate)[1, :1] + (y[:, unstriped(pos3)] - yc) * f64(gate)[2, :1] + (y[:, unstriped(pos4)] - yc) * f64(gate)[3, :1]
    return (out_0,) + planes(out_0)

from contextlib import ExitStack

import concourse.mybir as mybir
from concourse.masks import make_identity

K, T, S, D, V, N = 512, 1024, 512, 4, 256, 512
P = 128
FLOPS = 2 * K * N * S

F32 = mybir.dt.float32
BF16 = mybir.dt.bfloat16
I32 = mybir.dt.int32
U32 = mybir.dt.uint32
U16 = mybir.dt.uint16
U8 = mybir.dt.uint8
FP8X4 = mybir.dt.float8_e4m3fn_x4
MULT = mybir.AluOpType.mult
ADD = mybir.AluOpType.add
COPY = mybir.ActivationFunctionType.Copy

RAW = [3]


def tile_picked_grand_none_po_kernel(
    tc, x_words, x_scales, w1, gate, offs, cen, pos1, pos2, pos3, pos4, out_0, out_1, out_2
):
    nc = tc.nc
    with ExitStack() as ctx:
        keep = ctx.enter_context(tc.tile_pool(name="keep", bufs=1))
        ring = ctx.enter_context(tc.tile_pool(name="ring", bufs=4))
        rot = ctx.enter_context(tc.psum_pool(name="rot", bufs=4))
        accp = ctx.enter_context(tc.psum_pool(name="accp", bufs=2))

        offs_sb = keep.tile([P, S // 16], U16, name="offs_sb")
        xs_sb = keep.tile([P, T], U8, name="xs_sb", align_bytes=64)
        xw_sb = keep.tile([P, T], I32, name="xw_sb", tag="second", align_bytes=64)
        w_raw = [keep.tile([P, 4, 256], F32, name="w_raw%d" % c) for c in range(2)]
        zero = keep.tile([P, 1], F32, name="zero")
        nc.gpsimd.memset(zero[:], 0.0)
        nc.gpsimd.memset(xs_sb[:].bitcast(I32), 0)
        w_rows = w1.rearrange("(p j) n -> p j n", j=4)
        nc.sync.dma_start(offs_sb[:], offs)
        nc.sync.dma_start(w_raw[0][:, 0:2, :], w_rows[:, 0:2, 0:256])
        for q in range(4):
            nc.sync.dma_start(xs_sb[32 * q : 32 * q + 4, :].bitcast(I32), x_scales[0, 4 * q : 4 * q + 4, :].bitcast(I32))
        nc.sync.dma_start(w_raw[0][:, 2:4, :], w_rows[:, 2:4, 0:256])
        nc.sync.dma_start(xw_sb[:], x_words[0].rearrange("p c r -> p (c r)").bitcast(I32))
        nc.sync.dma_start(w_raw[1][:], w_rows[:, :, 256:512])

        order = [pos1, pos2, pos3, cen, pos4]
        gate_of = [0, 1, 2, None, 3]
        lists = [keep.tile([P, V // 16], U16, name="list%d" % i) for i in range(5)]
        gate0 = keep.tile([P, V], F32, name="gate0")
        gate123 = keep.tile([P, 3, V], F32, name="gate123")
        gate_sb = [gate0[:], gate123[:, 0, :], gate123[:, 1, :], gate123[:, 2, :]]
        gates = {i: gate_sb[gate_of[i]] for i in range(5) if gate_of[i] is not None}
        nc.sync.dma_start(lists[0][:], order[0])
        nc.sync.dma_start(gate0[:], gate[0])
        nc.sync.dma_start(lists[1][:], order[1])
        nc.sync.dma_start(gate123[:], gate[1:4].rearrange("d p v -> p d v"))
        for i in range(2, 5):
            nc.sync.dma_start(lists[i][:], order[i])

        ident = keep.tile([P, P], F32, name="ident")
        make_identity(nc, ident[:])
        one = keep.tile([P, 1], F32, name="one")
        nc.scalar.activation(one[:], zero[:], COPY, bias=1.0)

        xs_g = keep.tile([P, S], U8, name="xs_g", align_bytes=64)
        nc.vector.tensor_copy(xs_g[:], xs_sb[:].indirect(offs_sb[:]))

        y = [keep.tile([P, S], F32, name="y%d" % u) for u in range(4)]
        w_src = [w_raw[c][:].rearrange("p j (i s e) -> p s i j e", s=2, e=2) for c in range(2)]

        def quant(wb, cols, name):
            codes = keep.tile([P, cols], U32, name=name + "c", align_bytes=64)
            scales = keep.tile([P, cols], U8, name=name + "s", align_bytes=64)
            nc.vector.quantize_mx(out=codes[:].bitcast(FP8X4), scales=scales[:], in_=wb[:])
            return codes, scales

        def product(u, codes, scales, lo, hi):
            bank = rot.tile([P, 512], F32, name="bank", tag="bank")
            nc.tensor.matmul_mx(out=bank[:, 0 : hi - lo], lhsT=codes.bitcast(FP8X4), lhsT_scale=scales,
                                rhs=xw_g[:, lo:hi].bitcast(FP8X4), rhs_scale=xs_g[:, lo:hi], start=True, stop=True)
            nc.scalar.copy(y[u][:, lo:hi], bank[:, 0 : hi - lo])
            return bank

        wb0 = keep.tile([P, 512], BF16, name="wb0", tag="first", align_bytes=64)
        nc.scalar.activation(wb0[:].rearrange("p (e i j) -> p i j e", e=2, j=4), w_src[0][:, 0], COPY)
        c0 = keep.tile([P, P], U32, name="c0", tag="third", align_bytes=64)
        s0 = keep.tile([P, P], U8, name="s0", align_bytes=64)
        nc.vector.quantize_mx(out=c0[:].bitcast(FP8X4), scales=s0[:], in_=wb0[:])

        xw_g = keep.tile([P, S], U32, name="xw_g", tag="first", align_bytes=64)
        for lo, hi in ((0, 256), (256, 384), (384, 512)):
            nc.vector.tensor_copy(xw_g[:, lo:hi], xw_sb[:].bitcast(U32).indirect(offs_sb[:, lo // 16 : hi // 16]))
            last_bank = product(0, c0[:], s0[:], lo, hi)
        wb1 = keep.tile([P, 512], BF16, name="wb1", tag="second", align_bytes=64)
        nc.vector.tensor_copy(wb1[:].rearrange("p (e i j) -> p i j e", e=2, j=4), w_src[1][:, 0])
        c1, s1 = quant(wb1, 128, "wq1")
        product(1, c1[:], s1[:], 0, 512)
        acc01 = accp.tile([P, 2, 2, P], F32, name="acc", tag="acc")
        for i, tag in ((0, "second"), (1, "third")):
            g0 = keep.tile([P, V], F32, name="g0", tag=tag, align_bytes=64)
            nc.vector.tensor_tensor(g0[:], y[0][:].indirect(lists[i][:]), gates[i], MULT)
            for h in range(2):
                nc.tensor.matmul(acc01[:, h, 0, :], g0[:, P * h : P * h + P], ident[:], is_transpose=True, start=(i + h == 0), stop=False)
        wb23 = keep.tile([P, 1024], BF16, name="wb23", tag="third", align_bytes=64)
        wb23_v = wb23[:].rearrange("p (e c i j) -> p c i j e", e=2, c=2, j=4)
        for c in range(2):
            nc.scalar.copy(wb23_v[:, c], w_src[c][:, 1])
        c23, s23 = quant(wb23, 256, "wq23")

        gq = last_bank[:, 128:384].rearrange("p (h c) -> p h c", h=2)
        cself = keep.tile([P, 2], F32, name="cself")
        for h in range(2):
            for d in range(4):
                nc.tensor.matmul(gq[:, h, :], gate_sb[d][:, P * h : P * h + P], ident[:], is_transpose=True, start=(d == 0), stop=(d == 3))
        nc.scalar.activation(cself[:], gq[:, :, 0], mybir.ActivationFunctionType.Identity, bias=one[:], scale=-1.0)

        product(3, c23[:, 128:256], s23[:, 128:256], 0, 512)
        product(2, c23[:, 0:128], s23[:, 0:128], 0, 512)

        def scale_of(i, h):
            if gate_of[i] is None:
                return cself[:, h : h + 1]
            return None

        def gather(u, i, raw):
            if (u, i) == (1, 1):
                g = keep.tile([P, V], F32, name="g", tag="third", align_bytes=64)
            else:
                g = ring.tile([P, V], F32, name="g", tag="g", bufs=6)
            if raw:
                nc.vector.tensor_copy(g[:], y[u][:].indirect(lists[i][:]))
            else:
                nc.vector.tensor_tensor(g[:], y[u][:].indirect(lists[i][:]), gates[i], MULT)
            return g

        o = keep.tile([P, 4, V], F32, name="o")
        out_rows = out_0.rearrange("(p t) v -> p t v", t=4)

        def through_psum(us, idxs):
            nu = len(us)
            fused = [i for i in idxs if i not in RAW]
            raws = [i for i in idxs if i in RAW]
            fin = accp.tile([P, nu, V], F32, name="fin", tag="fin")
            nback = len(raws) + (1 if fused else 0)
            if nu == 2:
                acc = acc01
            else:
                acc = accp.tile([P, 2, nu, P], F32, name="acc", tag="acc")
            turned = {}
            banks = {}
            state = {"fwd": 4 if nu == 2 else 0, "back": 0}

            def back(tt):
                for e in range(nu):
                    for h in range(2):
                        n = state["back"]
                        nc.tensor.matmul(fin[:, e, P * h : P * h + P], tt[:, h, e, :], ident[:], is_transpose=True,
                                         start=(n == 0), stop=(n == nback * nu * 2 - 1))
                        state["back"] = n + 1

            def views(bank, tt, h):
                if nu == 2:
                    return (tt[:, h].rearrange("p e (c i) -> p c e i", c=2), bank[:, h].rearrange("p c (e i) -> p c e i", e=2))
                return tt[:, h], bank[:, h]

            for c, u in enumerate(us):
                for i in idxs:
                    if u == 0 and i < 2:
                        continue
                    g = gather(u, i, i in RAW)
                    if i in RAW:
                        if c == 0:
                            turned[i] = ring.tile([P, 2, nu, P], F32, name="tt", tag="tt", bufs=6)
                        bank = rot.tile([P, 2, P], F32, name="rb", tag="bank")
                        for h in range(2):
                            nc.tensor.transpose(bank[:, h, :], g[:, P * h : P * h + P], ident[:])
                        for h in range(2):
                            if nu == 2:
                                dst = turned[i][:, h].rearrange("p e (c i) -> p c e i", c=2)[:, c]
                                src = bank[:, h, :].rearrange("p (e i) -> p e i", e=2)
                            else:
                                dst = turned[i][:, h, 0, :]
                                src = bank[:, h, :]
                            nc.scalar.activation(dst, src, COPY, scale=scale_of(i, h))
                        if c == nu - 1:
                            back(turned[i])
                    else:
                        for h in range(2):
                            n = state["fwd"]
                            nc.tensor.matmul(acc[:, h, c, :], g[:, P * h : P * h + P], ident[:], is_transpose=True,
                                             start=(n == 0), stop=(n == len(fused) * nu * 2 - 1))
                            state["fwd"] = n + 1
            if fused:
                tt = ring.tile([P, 2, nu, P], F32, name="tt", tag="tt", bufs=6)
                if nu == 2:
                    for h in range(2):
                        dst, src = views(acc, tt, h)
                        nc.scalar.copy(dst, src)
                else:
                    nc.scalar.copy(tt[:], acc[:])
                back(tt)
            return fin

        fin01 = through_psum([0, 1], [0, 1, 2, 3, 4])
        nc.scalar.copy(o[:, 0:2, :], fin01[:])
        nc.sync.dma_start(out_rows[:, 0:2, :], o[:, 0:2, :])
        ob = keep.tile([P, 4 * V], BF16, name="ob", align_bytes=64)
        ob_v = ob[:].rearrange("p (c i s e) -> p s c i e", i=4, s=2, e=2)
        o_v = o[:].rearrange("p (s e) (c i) -> p s c i e", i=4, s=2)
        nc.scalar.copy(ob_v[:, 0], o_v[:, 0])
        fin3 = through_psum([3], [0, 1, 2, 3])
        fin2 = through_psum([2], [0, 1, 2, 3])
        for t, fin in ((3, fin3), (2, fin2)):
            g = gather(t, 4, False)
            nc.vector.tensor_tensor(o[:, t, :], g[:], fin[:, 0, :], ADD)
            nc.sync.dma_start(out_rows[:, t, :], o[:, t, :])

        nc.vector.tensor_copy(ob_v[:, 1], o_v[:, 1])
        oc, os_ = quant(ob, V, "oq")
        nc.sync.dma_start(out_1[0].rearrange("p c r -> p (c r)").bitcast(I32), oc[:].bitcast(I32))
        for q in range(4):
            eng = nc.scalar if q % 2 == 0 else nc.sync
            eng.dma_start(out_2[0, 4 * q : 4 * q + 4, :].bitcast(I32), os_[32 * q : 32 * q + 4, :].bitcast(I32))
